import numpy as np
import ml_dtypes


def mxq(x, axis, fmt="e4m3"):
    dtype, down = {"e4m3": (ml_dtypes.float8_e4m3fn, 7), "e5m2": (ml_dtypes.float8_e5m2, 14)}[fmt]
    v = np.moveaxis(np.asarray(x, np.float32).astype(ml_dtypes.bfloat16).astype(np.float64), axis, -1)
    blocks = v.reshape(v.shape[:-1] + (-1, 32))
    amax = np.abs(blocks).max(-1, keepdims=True)
    byte = np.maximum(np.where(amax > 0, np.frexp(amax)[1] - 1 + 127, 0) - down, 1)
    scale = np.exp2(byte - 127.0)
    codes = (blocks / scale).astype(np.float32).astype(dtype).astype(np.float64)
    return np.moveaxis((codes * scale).reshape(v.shape), -1, axis)


WIDE = False


def mx_kscale(k):
    if not WIDE:
        return np.ones(k)
    levels = np.array([30, -30])
    if k % 512:
        return np.exp2(np.random.permutation(np.resize(levels, k // 32))).repeat(32)
    a = np.empty((k // 512, 16))
    for p in range(k // 512):
        a[p, :8] = np.random.permutation(np.resize(levels, 8))
        for g in range(8):
            far = levels[np.abs(levels - a[p, g]) >= 10]
            a[p, g + 8] = far[np.random.randint(len(far))]
    return np.exp2(a.ravel()).repeat(32)


def f64(x):
    return np.asarray(x).astype(np.float64)


def striped(idx):
    return np.tile(np.asarray(idx).reshape(-1, 16).T, (8, 1)).astype(np.uint16)


def unstriped(offs):
    return offs[:16].T.reshape(-1).astype(np.int64)


E2M1 = np.array([0.0, 0.5, 1.0, 1.5, 2.0, 3.0, 4.0, 6.0, -0.0, -0.5, -1.0, -1.5, -2.0, -3.0, -4.0, -6.0])


def pack_weight(w, fmt):
    k, n = w.shape
    w = f64(np.asarray(w, np.float32).astype(ml_dtypes.bfloat16)).reshape(k // 32, 32, n)
    amax = np.abs(w).max(1)
    if fmt == "e4m3":
        byte = np.frexp(amax)[1] - 1 + 127 - 7
    else:
        mant, ex = np.frexp(amax / 6.0)
        byte = np.where(mant > 0.5, ex, ex - 1) + 127
    byte = np.clip(np.where(amax > 0, byte, 1), 1, 254)
    scaled = (w * np.exp2(127.0 - byte)[:, None, :]).reshape(k, n).astype(np.float32)
    by_word = np.ascontiguousarray(scaled.reshape(k // 512, 128, 4, n).transpose(0, 1, 3, 2))
    if fmt == "e4m3":
        words = by_word.astype(ml_dtypes.float8_e4m3fn).view(np.uint8)
    else:
        c = by_word.astype(ml_dtypes.float4_e2m1fn).view(np.uint8) & 0xF
        words = (c[..., 0::2] | (c[..., 1::2] << 4)).reshape(k // 512, 128, 2 * n)
    return np.ascontiguousarray(words), np.ascontiguousarray(byte.astype(np.uint8).reshape(k // 512, 16, n))


def unpack_weight(words, scales, fmt):
    g, _, n = scales.shape
    words = np.ascontiguousarray(words).reshape(g, 128, n, -1)
    if fmt == "e4m3":
        vals = words.view(ml_dtypes.float8_e4m3fn).astype(np.float64)
    else:
        nib = np.empty((g, 128, n, 4), np.uint8)
        nib[..., 0::2] = words & 0xF
        nib[..., 1::2] = words >> 4
        vals = E2M1[nib]
    vals = vals * np.repeat(np.exp2(scales.astype(np.float64) - 127.0), 8, axis=1)[..., None]
    return vals.transpose(0, 1, 3, 2).reshape(g * 512, n)


K, N, M, T, J = 512, 512, 512, 512, 512


def setup_inputs():
    n = np.random.standard_normal
    idx = np.random.randint(0, T, J)
    fk = mx_kscale(K)
    fn = mx_kscale(N)
    xtp = pack_weight(n((K, T)) / fk[:, None], "e4m3")
    wp = pack_weight(n((K, N)) * 1 / np.sqrt(K) * fk[:, None] * fn, "e2m1")
    wbp = pack_weight(n((N, M)) * 1 / np.sqrt(N) / fn[:, None], "e4m3")
    return {
        "xt_words": xtp[0],
        "xt_scales": xtp[1],
        "w_words": wp[0],
        "w_scales": wp[1],
        "g": (1.0 * n((N, J))).astype(np.float32),
        "wb_words": wbp[0],
        "wb_scales": wbp[1],
        "offs": striped(idx),
    }


def reference(xt_words, xt_scales, w_words, w_scales, g, wb_words, wb_scales, offs):
    idx = unstriped(offs)
    xtu = unpack_weight(xt_words, xt_scales, "e4m3")
    wu = unpack_weight(w_words, w_scales, "e2m1")
    wbu = unpack_weight(wb_words, wb_scales, "e4m3")
    z = wu.T @ xtu
    d = f64(g) * z[:, idx]
    dq = mxq(d, 0, "e5m2")
    y = wbu.T @ dq
    return y

@@ -1,0 +1,123 @@
+from contextlib import ExitStack
+
+import concourse.mybir as mybir
+
+K, N, M, T, J = 512, 512, 512, 512, 512
+FLOPS = 2 * K * N * T + 2 * N * M * J
+
+F32 = mybir.dt.float32
+BF16 = mybir.dt.bfloat16
+I32 = mybir.dt.int32
+U32 = mybir.dt.uint32
+U16 = mybir.dt.uint16
+U8 = mybir.dt.uint8
+E4M3 = mybir.dt.float8_e4m3fn_x4
+E5M2 = mybir.dt.float8_e5m2_x4
+E2M1 = mybir.dt.float4_e2m1fn_x4
+MULT = mybir.AluOpType.mult
+
+P = 128
+PACK = 4
+CHUNKS = (256, 128, 64, 64)
+G_COLS = 256
+HALF = T // 2
+
+
+def load_scale_rows(queues, plane, scales):
+    for q in range(4):
+        queues[q].dma_start(out=plane[32 * q : 32 * q + 4, :].bitcast(I32), in_=scales[0, 4 * q : 4 * q + 4, :].bitcast(I32))
+
+
+def tile_list_pair_product_back_kernel(tc, xt_words, xt_scales, w_words, w_scales, g, wb_words, wb_scales, offs, out):
+    nc = tc.nc
+    with ExitStack() as ctx:
+        sb = ctx.enter_context(tc.tile_pool(name="sb", bufs=1))
+        ps = ctx.enter_context(tc.psum_pool(name="ps", bufs=1))
+
+        offsets = sb.tile([P, J // 16], U16, name="offsets")
+        w_raw = sb.tile([P, 2 * N], U8, name="w_raw", align_bytes=64)
+        ws_raw = sb.tile([P, N], U8, name="ws_raw", align_bytes=64)
+        x_codes = sb.tile([P, T], U32, name="x_codes", align_bytes=64)
+        x_plane = sb.tile([P, T], U8, name="x_plane", align_bytes=64)
+        wb_codes = sb.tile([P, M], U32, name="wb_codes", align_bytes=64)
+        wb_plane = sb.tile([P, M], U8, name="wb_plane", align_bytes=64)
+        warm_in = sb.tile([P, 8], F32, name="warm_in")
+        warm_out = sb.tile([P, 8], F32, name="warm_out")
+
+        nc.vector.memset(ws_raw[:].bitcast(I32), 0)
+        nc.vector.memset(x_plane[:].bitcast(I32), 0)
+        nc.vector.memset(wb_plane[:].bitcast(I32), 0)
+        nc.vector.memset(warm_in[:], 0.0)
+
+        nc.sync.dma_start(out=w_raw[:].bitcast(I32), in_=w_words[0].bitcast(I32))
+        nc.scalar.dma_start(out=x_codes[:].bitcast(I32), in_=xt_words[0].rearrange("p c r -> p (c r)").bitcast(I32))
+        load_scale_rows([nc.sync] * 4, ws_raw, w_scales)
+        load_scale_rows([nc.scalar, nc.scalar, nc.sync, nc.sync], x_plane, xt_scales)
+        nc.scalar.copy(out=warm_out[:], in_=warm_in[:])
+        g_rows = g.rearrange("(p t) j -> p t j", t=PACK)
+        g_tiles = {}
+        for h, t0, nt in ((0, 0, 2), (0, 2, 2), (1, 0, 4)):
+            g_tile = sb.tile([P, nt, G_COLS], F32, name=f"g{h}{t0}")
+            nc.sync.dma_start(out=g_tile[:], in_=g_rows[:, t0 : t0 + nt, h * G_COLS : (h + 1) * G_COLS])
+            for t in range(nt):
+                g_tiles[h, t0 + t] = g_tile[:, t, :]
+            if (h, t0) == (0, 0):
+                nc.sync.dma_start(offsets[:], offs)
+        nc.sync.dma_start(out=wb_codes[:].bitcast(I32), in_=wb_words[0].rearrange("p c r -> p (c r)").bitcast(I32))
+        load_scale_rows([nc.sync] * 4, wb_plane, wb_scales)
+
+        z_tiles = []
+        w_by_t = w_raw[:].bitcast(U16).rearrange("p (q t) -> p t q", t=PACK)
+        ws_by_t = ws_raw[:].rearrange("p (q t) -> p t q", t=PACK)
+        for t in range(PACK):
+            w_t = sb.tile([P, 2 * P], U8, name=f"w_t{t}", align_bytes=64)
+            ws_t = sb.tile([P, P], U8, name=f"ws_t{t}", align_bytes=64)
+            nc.vector.tensor_copy(out=w_t[:].bitcast(U16), in_=w_by_t[:, t, :])
+            nc.vector.tensor_copy(out=ws_t[:], in_=ws_by_t[:, t, :])
+            z_t = sb.tile([P, T], F32, name=f"z{t}")
+            for h in range(2):
+                cols = slice(h * HALF, (h + 1) * HALF)
+                z_bank = ps.tile([P, HALF], F32, name=f"z_bank{t}{h}", tag=f"bank{2 * t + h}")
+                nc.tensor.matmul_mx(z_bank[:], lhsT=w_t[:].bitcast(E2M1), lhsT_scale=ws_t[:],
+                                    rhs=x_codes[:, cols].bitcast(E4M3), rhs_scale=x_plane[:, cols], start=True, stop=True)
+                nc.scalar.copy(out=z_t[:, cols], in_=z_bank[:])
+            z_tiles.append(z_t)
+
+        d_codes = sb.tile([P, J], U32, name="d_codes", align_bytes=64)
+        d_plane = sb.tile([P, J], U8, name="d_plane", align_bytes=64)
+
+        def gather(c, j0, width):
+            d32 = sb.tile([P, PACK, width], F32, name=f"d32_{c}")
+            h, g0 = divmod(j0, G_COLS)
+            for t in range(PACK):
+                nc.vector.tensor_tensor(d32[:, t, :], z_tiles[t][:].indirect(offsets[:, j0 // 16 : (j0 + width) // 16]),
+                                        g_tiles[h, t][:, g0 : g0 + width], MULT)
+            d16 = sb.tile([P, width, PACK], BF16, name=f"d16_{c}", align_bytes=64)
+            nc.scalar.copy(out=d16[:].rearrange("p (c i) t -> p c t i", i=4), in_=d32[:].rearrange("p t (c i) -> p c t i", i=4))
+            return d16
+
+        def quantise(j0, width, d16):
+            nc.vector.quantize_mx(out=d_codes[:, j0 : j0 + width].bitcast(E5M2), scales=d_plane[:, j0 : j0 + width],
+                                  in_=d16[:].rearrange("p j t -> p (j t)"))
+
+        pending = None
+        j0 = 0
+        for c, width in enumerate(CHUNKS):
+            d16 = gather(c, j0, width)
+            if pending is not None:
+                quantise(*pending)
+            pending = (j0, width, d16)
+            j0 += width
+        quantise(*pending)
+
+        for mt in range(M // P):
+            cols = slice(mt * P, (mt + 1) * P)
+            y_bank = ps.tile([P, J], F32, name=f"y_bank{mt}", tag=f"bank{mt}")
+            nc.tensor.matmul_mx(y_bank[:], lhsT=wb_codes[:, cols].bitcast(E4M3), lhsT_scale=wb_plane[:, cols],
+                                rhs=d_codes[:].bitcast(E5M2), rhs_scale=d_plane[:], start=True, stop=True)
+            y = sb.tile([P, J], F32, name=f"y{mt}")
+            if mt % 2 == 0:
+                nc.scalar.copy(out=y[:], in_=y_bank[:])
+            else:
+                nc.vector.tensor_copy(out=y[:], in_=y_bank[:])
+            nc.sync.dma_start(out=out[cols, :], in_=y[:])

@@ -23,9 +23,12 @@ G_COLS = 256
 HALF = T // 2
 
 
-def load_scale_rows(queues, plane, scales):
-    for q in range(4):
-        queues[q].dma_start(out=plane[32 * q : 32 * q + 4, :].bitcast(I32), in_=scales[0, 4 * q : 4 * q + 4, :].bitcast(I32))
+def load_scale_rows(nc, plane, scales, quadrants, copies=1):
+    for q in quadrants:
+        rows = scales[0, 4 * q : 4 * q + 4, :].bitcast(I32)
+        if copies > 1:
+            rows = rows.unsqueeze(0).broadcast_to([copies, 4, rows.shape[1]])
+        nc.sync.dma_start(out=plane[32 * q : 32 * q + 4 * copies, :].bitcast(I32), in_=rows)
 
 
 def tile_list_pair_product_back_kernel(tc, xt_words, xt_scales, w_words, w_scales, g, wb_words, wb_scales, offs, out):
@@ -44,15 +47,15 @@ def tile_list_pair_product_back_kernel(tc, xt_words, xt_scales, w_words, w_scale
         warm_in = sb.tile([P, 8], F32, name="warm_in")
         warm_out = sb.tile([P, 8], F32, name="warm_out")
 
-        nc.vector.memset(ws_raw[:].bitcast(I32), 0)
         nc.vector.memset(x_plane[:].bitcast(I32), 0)
-        nc.vector.memset(wb_plane[:].bitcast(I32), 0)
         nc.vector.memset(warm_in[:], 0.0)
+        nc.vector.memset(wb_plane[:].bitcast(I32), 0)
 
+        load_scale_rows(nc, ws_raw, w_scales, range(4), copies=8)
         nc.sync.dma_start(out=w_raw[:].bitcast(I32), in_=w_words[0].bitcast(I32))
-        nc.scalar.dma_start(out=x_codes[:].bitcast(I32), in_=xt_words[0].rearrange("p c r -> p (c r)").bitcast(I32))
-        load_scale_rows([nc.sync] * 4, ws_raw, w_scales)
-        load_scale_rows([nc.scalar, nc.scalar, nc.sync, nc.sync], x_plane, xt_scales)
+        load_scale_rows(nc, x_plane, xt_scales, range(2))
+        nc.sync.dma_start(out=x_codes[:].bitcast(I32), in_=xt_words[0].rearrange("p c r -> p (c r)").bitcast(I32))
+        load_scale_rows(nc, x_plane, xt_scales, range(2, 4))
         nc.scalar.copy(out=warm_out[:], in_=warm_in[:])
         g_rows = g.rearrange("(p t) j -> p t j", t=PACK)
         g_tiles = {}
@@ -64,9 +67,10 @@ def tile_list_pair_product_back_kernel(tc, xt_words, xt_scales, w_words, w_scale
             if (h, t0) == (0, 0):
                 nc.sync.dma_start(offsets[:], offs)
         nc.sync.dma_start(out=wb_codes[:].bitcast(I32), in_=wb_words[0].rearrange("p c r -> p (c r)").bitcast(I32))
-        load_scale_rows([nc.sync] * 4, wb_plane, wb_scales)
+        load_scale_rows(nc, wb_plane, wb_scales, range(4))
 
         z_tiles = []
+        banks_used = []
         w_by_t = w_raw[:].bitcast(U16).rearrange("p (q t) -> p t q", t=PACK)
         ws_by_t = ws_raw[:].rearrange("p (q t) -> p t q", t=PACK)
         for t in range(PACK):
@@ -75,9 +79,11 @@ def tile_list_pair_product_back_kernel(tc, xt_words, xt_scales, w_words, w_scale
             nc.vector.tensor_copy(out=w_t[:].bitcast(U16), in_=w_by_t[:, t, :])
             nc.vector.tensor_copy(out=ws_t[:], in_=ws_by_t[:, t, :])
             z_t = sb.tile([P, T], F32, name=f"z{t}")
-            for h in range(2):
-                cols = slice(h * HALF, (h + 1) * HALF)
-                z_bank = ps.tile([P, HALF], F32, name=f"z_bank{t}{h}", tag=f"bank{2 * t + h}")
+            width = T // 4 if t == 0 else T // 2
+            for c0 in range(0, T, width):
+                cols = slice(c0, c0 + width)
+                z_bank = ps.tile([P, width], F32, name=f"z_bank{t}_{c0}", tag=f"bank{len(banks_used) % 8}")
+                banks_used.append(t)
                 nc.tensor.matmul_mx(z_bank[:], lhsT=w_t[:].bitcast(E2M1), lhsT_scale=ws_t[:],
                                     rhs=x_codes[:, cols].bitcast(E4M3), rhs_scale=x_plane[:, cols], start=True, stop=True)
                 nc.scalar.copy(out=z_t[:, cols], in_=z_bank[:])
@@ -112,12 +118,15 @@ def tile_list_pair_product_back_kernel(tc, xt_words, xt_scales, w_words, w_scale
 
         for mt in range(M // P):
             cols = slice(mt * P, (mt + 1) * P)
-            y_bank = ps.tile([P, J], F32, name=f"y_bank{mt}", tag=f"bank{mt}")
+            y_bank = ps.tile([P, J], F32, name=f"y_bank{mt}", tag=f"bank{mt + 2}")
             nc.tensor.matmul_mx(y_bank[:], lhsT=wb_codes[:, cols].bitcast(E4M3), lhsT_scale=wb_plane[:, cols],
                                 rhs=d_codes[:].bitcast(E5M2), rhs_scale=d_plane[:], start=True, stop=True)
             y = sb.tile([P, J], F32, name=f"y{mt}")
-            if mt % 2 == 0:
-                nc.scalar.copy(out=y[:], in_=y_bank[:])
-            else:
-                nc.vector.tensor_copy(out=y[:], in_=y_bank[:])
-            nc.sync.dma_start(out=out[cols, :], in_=y[:])
+            width = J // 2 if mt in (0, M // P - 1) else J
+            for c0 in range(0, J, width):
+                piece = slice(c0, c0 + width)
+                if mt % 2 == 0:
+                    nc.scalar.copy(out=y[:, piece], in_=y_bank[:, piece])
+                else:
+                    nc.vector.tensor_copy(out=y[:, piece], in_=y_bank[:, piece])
+                nc.sync.dma_start(out=out[cols, piece], in_=y[:, piece])

@@ -51,11 +51,11 @@ def tile_list_pair_product_back_kernel(tc, xt_words, xt_scales, w_words, w_scale
         nc.vector.memset(warm_in[:], 0.0)
         nc.vector.memset(wb_plane[:].bitcast(I32), 0)
 
-        load_scale_rows(nc, ws_raw, w_scales, range(4), copies=8)
+        load_scale_rows(nc, ws_raw, w_scales, range(2), copies=8)
         nc.sync.dma_start(out=w_raw[:].bitcast(I32), in_=w_words[0].bitcast(I32))
-        load_scale_rows(nc, x_plane, xt_scales, range(2))
         nc.sync.dma_start(out=x_codes[:].bitcast(I32), in_=xt_words[0].rearrange("p c r -> p (c r)").bitcast(I32))
-        load_scale_rows(nc, x_plane, xt_scales, range(2, 4))
+        load_scale_rows(nc, ws_raw, w_scales, range(2, 4), copies=8)
+        load_scale_rows(nc, x_plane, xt_scales, range(4))
         nc.scalar.copy(out=warm_out[:], in_=warm_in[:])
         g_rows = g.rearrange("(p t) j -> p t j", t=PACK)
         g_tiles = {}
@@ -122,9 +122,9 @@ def tile_list_pair_product_back_kernel(tc, xt_words, xt_scales, w_words, w_scale
             nc.tensor.matmul_mx(y_bank[:], lhsT=wb_codes[:, cols].bitcast(E4M3), lhsT_scale=wb_plane[:, cols],
                                 rhs=d_codes[:].bitcast(E5M2), rhs_scale=d_plane[:], start=True, stop=True)
             y = sb.tile([P, J], F32, name=f"y{mt}")
-            width = J // 2 if mt in (0, M // P - 1) else J
-            for c0 in range(0, J, width):
-                piece = slice(c0, c0 + width)
+            edges = (0, 256, J)
+            for c0, c1 in zip(edges, edges[1:]):
+                piece = slice(c0, c1)
                 if mt % 2 == 0:
                     nc.scalar.copy(out=y[:, piece], in_=y_bank[:, piece])
                 else:

@@ -18,8 +18,8 @@ MULT = mybir.AluOpType.mult
 
 P = 128
 PACK = 4
-CHUNKS = (256, 128, 64, 64)
-G_COLS = 256
+CHUNKS = (288, 160, 64)
+QUANT = (256, 128, 64, 64)
 HALF = T // 2
 
 
@@ -59,12 +59,13 @@ def tile_list_pair_product_back_kernel(tc, xt_words, xt_scales, w_words, w_scale
         nc.scalar.copy(out=warm_out[:], in_=warm_in[:])
         g_rows = g.rearrange("(p t) j -> p t j", t=PACK)
         g_tiles = {}
-        for h, t0, nt in ((0, 0, 2), (0, 2, 2), (1, 0, 4)):
-            g_tile = sb.tile([P, nt, G_COLS], F32, name=f"g{h}{t0}")
-            nc.sync.dma_start(out=g_tile[:], in_=g_rows[:, t0 : t0 + nt, h * G_COLS : (h + 1) * G_COLS])
+        first = CHUNKS[0]
+        for j0, j1, t0, nt in ((0, first, 0, 2), (0, first, 2, 2), (first, J, 0, 4)):
+            g_tile = sb.tile([P, nt, j1 - j0], F32, name=f"g{j0}_{t0}")
+            nc.sync.dma_start(out=g_tile[:], in_=g_rows[:, t0 : t0 + nt, j0:j1])
             for t in range(nt):
-                g_tiles[h, t0 + t] = g_tile[:, t, :]
-            if (h, t0) == (0, 0):
+                g_tiles[j0, t0 + t] = g_tile[:, t, :]
+            if (j0, t0) == (0, 0):
                 nc.sync.dma_start(offsets[:], offs)
         nc.sync.dma_start(out=wb_codes[:].bitcast(I32), in_=wb_words[0].rearrange("p c r -> p (c r)").bitcast(I32))
         load_scale_rows(nc, wb_plane, wb_scales, range(4))
@@ -92,29 +93,22 @@ def tile_list_pair_product_back_kernel(tc, xt_words, xt_scales, w_words, w_scale
         d_codes = sb.tile([P, J], U32, name="d_codes", align_bytes=64)
         d_plane = sb.tile([P, J], U8, name="d_plane", align_bytes=64)
 
-        def gather(c, j0, width):
-            d32 = sb.tile([P, PACK, width], F32, name=f"d32_{c}")
-            h, g0 = divmod(j0, G_COLS)
-            for t in range(PACK):
-                nc.vector.tensor_tensor(d32[:, t, :], z_tiles[t][:].indirect(offsets[:, j0 // 16 : (j0 + width) // 16]),
-                                        g_tiles[h, t][:, g0 : g0 + width], MULT)
-            d16 = sb.tile([P, width, PACK], BF16, name=f"d16_{c}", align_bytes=64)
-            nc.scalar.copy(out=d16[:].rearrange("p (c i) t -> p c t i", i=4), in_=d32[:].rearrange("p t (c i) -> p c t i", i=4))
-            return d16
-
-        def quantise(j0, width, d16):
-            nc.vector.quantize_mx(out=d_codes[:, j0 : j0 + width].bitcast(E5M2), scales=d_plane[:, j0 : j0 + width],
-                                  in_=d16[:].rearrange("p j t -> p (j t)"))
-
-        pending = None
+        d16 = sb.tile([P, J * PACK], BF16, name="d16", align_bytes=64)
         j0 = 0
         for c, width in enumerate(CHUNKS):
-            d16 = gather(c, j0, width)
-            if pending is not None:
-                quantise(*pending)
-            pending = (j0, width, d16)
+            d32 = sb.tile([P, PACK, width], F32, name=f"d32_{c}")
+            base = 0 if j0 < first else first
+            for t in range(PACK):
+                nc.vector.tensor_tensor(d32[:, t, :], z_tiles[t][:].indirect(offsets[:, j0 // 16 : (j0 + width) // 16]),
+                                        g_tiles[base, t][:, j0 - base : j0 - base + width], MULT)
+            nc.scalar.copy(out=d16[:, PACK * j0 : PACK * (j0 + width)].rearrange("p (c i t) -> p c t i", i=4, t=PACK),
+                           in_=d32[:].rearrange("p t (c i) -> p c t i", i=4))
             j0 += width
-        quantise(*pending)
+        j0 = 0
+        for width in QUANT:
+            nc.vector.quantize_mx(out=d_codes[:, j0 : j0 + width].bitcast(E5M2), scales=d_plane[:, j0 : j0 + width],
+                                  in_=d16[:, PACK * j0 : PACK * (j0 + width)])
+            j0 += width
 
         for mt in range(M // P):
             cols = slice(mt * P, (mt + 1) * P)

from contextlib import ExitStack

import concourse.mybir as mybir

K, N, M, T, J = 512, 512, 512, 512, 512
FLOPS = 2 * K * N * T + 2 * N * M * J

F32 = mybir.dt.float32
BF16 = mybir.dt.bfloat16
I32 = mybir.dt.int32
U32 = mybir.dt.uint32
U16 = mybir.dt.uint16
U8 = mybir.dt.uint8
E4M3 = mybir.dt.float8_e4m3fn_x4
E5M2 = mybir.dt.float8_e5m2_x4
E2M1 = mybir.dt.float4_e2m1fn_x4
MULT = mybir.AluOpType.mult

P = 128
PACK = 4
CHUNKS = (288, 160, 64)
QUANT = (256, 128, 64, 64)
HALF = T // 2


def load_scale_rows(nc, plane, scales, quadrants, copies=1):
    for q in quadrants:
        rows = scales[0, 4 * q : 4 * q + 4, :].bitcast(I32)
        if copies > 1:
            rows = rows.unsqueeze(0).broadcast_to([copies, 4, rows.shape[1]])
        nc.sync.dma_start(out=plane[32 * q : 32 * q + 4 * copies, :].bitcast(I32), in_=rows)


def tile_list_pair_product_back_kernel(tc, xt_words, xt_scales, w_words, w_scales, g, wb_words, wb_scales, offs, out):
    nc = tc.nc
    with ExitStack() as ctx:
        sb = ctx.enter_context(tc.tile_pool(name="sb", bufs=1))
        ps = ctx.enter_context(tc.psum_pool(name="ps", bufs=1))

        offsets = sb.tile([P, J // 16], U16, name="offsets")
        w_raw = sb.tile([P, 2 * N], U8, name="w_raw", align_bytes=64)
        ws_raw = sb.tile([P, N], U8, name="ws_raw", align_bytes=64)
        x_codes = sb.tile([P, T], U32, name="x_codes", align_bytes=64)
        x_plane = sb.tile([P, T], U8, name="x_plane", align_bytes=64)
        wb_codes = sb.tile([P, M], U32, name="wb_codes", align_bytes=64)
        wb_plane = sb.tile([P, M], U8, name="wb_plane", align_bytes=64)
        warm_in = sb.tile([P, 8], F32, name="warm_in")
        warm_out = sb.tile([P, 8], F32, name="warm_out")

        nc.vector.memset(x_plane[:].bitcast(I32), 0)
        nc.vector.memset(warm_in[:], 0.0)
        nc.vector.memset(wb_plane[:].bitcast(I32), 0)

        load_scale_rows(nc, ws_raw, w_scales, range(2), copies=8)
        nc.sync.dma_start(out=w_raw[:].bitcast(I32), in_=w_words[0].bitcast(I32))
        nc.sync.dma_start(out=x_codes[:].bitcast(I32), in_=xt_words[0].rearrange("p c r -> p (c r)").bitcast(I32))
        load_scale_rows(nc, ws_raw, w_scales, range(2, 4), copies=8)
        load_scale_rows(nc, x_plane, xt_scales, range(4))
        nc.scalar.copy(out=warm_out[:], in_=warm_in[:])
        g_rows = g.rearrange("(p t) j -> p t j", t=PACK)
        g_tiles = {}
        first = CHUNKS[0]
        for j0, j1, t0, nt in ((0, first, 0, 2), (0, first, 2, 2), (first, J, 0, 4)):
            g_tile = sb.tile([P, nt, j1 - j0], F32, name=f"g{j0}_{t0}")
            nc.sync.dma_start(out=g_tile[:], in_=g_rows[:, t0 : t0 + nt, j0:j1])
            for t in range(nt):
                g_tiles[j0, t0 + t] = g_tile[:, t, :]
            if (j0, t0) == (0, 0):
                nc.sync.dma_start(offsets[:], offs)
        nc.sync.dma_start(out=wb_codes[:].bitcast(I32), in_=wb_words[0].rearrange("p c r -> p (c r)").bitcast(I32))
        load_scale_rows(nc, wb_plane, wb_scales, range(4))

        z_tiles = []
        banks_used = []
        w_by_t = w_raw[:].bitcast(U16).rearrange("p (q t) -> p t q", t=PACK)
        ws_by_t = ws_raw[:].rearrange("p (q t) -> p t q", t=PACK)
        for t in range(PACK):
            w_t = sb.tile([P, 2 * P], U8, name=f"w_t{t}", align_bytes=64)
            ws_t = sb.tile([P, P], U8, name=f"ws_t{t}", align_bytes=64)
            nc.vector.tensor_copy(out=w_t[:].bitcast(U16), in_=w_by_t[:, t, :])
            nc.vector.tensor_copy(out=ws_t[:], in_=ws_by_t[:, t, :])
            z_t = sb.tile([P, T], F32, name=f"z{t}")
            width = T // 4 if t == 0 else T // 2
            for c0 in range(0, T, width):
                cols = slice(c0, c0 + width)
                z_bank = ps.tile([P, width], F32, name=f"z_bank{t}_{c0}", tag=f"bank{len(banks_used) % 8}")
                banks_used.append(t)
                nc.tensor.matmul_mx(z_bank[:], lhsT=w_t[:].bitcast(E2M1), lhsT_scale=ws_t[:],
                                    rhs=x_codes[:, cols].bitcast(E4M3), rhs_scale=x_plane[:, cols], start=True, stop=True)
                nc.scalar.copy(out=z_t[:, cols], in_=z_bank[:])
            z_tiles.append(z_t)

        d_codes = sb.tile([P, J], U32, name="d_codes", align_bytes=64)
        d_plane = sb.tile([P, J], U8, name="d_plane", align_bytes=64)

        d16 = sb.tile([P, J * PACK], BF16, name="d16", align_bytes=64)
        j0 = 0
        for c, width in enumerate(CHUNKS):
            d32 = sb.tile([P, PACK, width], F32, name=f"d32_{c}")
            base = 0 if j0 < first else first
            for t in range(PACK):
                nc.vector.tensor_tensor(d32[:, t, :], z_tiles[t][:].indirect(offsets[:, j0 // 16 : (j0 + width) // 16]),
                                        g_tiles[base, t][:, j0 - base : j0 - base + width], MULT)
            nc.scalar.copy(out=d16[:, PACK * j0 : PACK * (j0 + width)].rearrange("p (c i t) -> p c t i", i=4, t=PACK),
                           in_=d32[:].rearrange("p t (c i) -> p c t i", i=4))
            j0 += width
        j0 = 0
        for width in QUANT:
            nc.vector.quantize_mx(out=d_codes[:, j0 : j0 + width].bitcast(E5M2), scales=d_plane[:, j0 : j0 + width],
                                  in_=d16[:, PACK * j0 : PACK * (j0 + width)])
            j0 += width

        for mt in range(M // P):
            cols = slice(mt * P, (mt + 1) * P)
            y_bank = ps.tile([P, J], F32, name=f"y_bank{mt}", tag=f"bank{mt + 2}")
            nc.tensor.matmul_mx(y_bank[:], lhsT=wb_codes[:, cols].bitcast(E4M3), lhsT_scale=wb_plane[:, cols],
                                rhs=d_codes[:].bitcast(E5M2), rhs_scale=d_plane[:], start=True, stop=True)
            y = sb.tile([P, J], F32, name=f"y{mt}")
            edges = (0, 256, J)
            for c0, c1 in zip(edges, edges[1:]):
                piece = slice(c0, c1)
                if mt % 2 == 0:
                    nc.scalar.copy(out=y[:, piece], in_=y_bank[:, piece])
                else:
                    nc.vector.tensor_copy(out=y[:, piece], in_=y_bank[:, piece])
                nc.sync.dma_start(out=out[cols, piece], in_=y[:, piece])
